import numpy as np
import ml_dtypes


def mxq(x, axis, fmt="e4m3"):
    dtype, down = {"e4m3": (ml_dtypes.float8_e4m3fn, 7), "e5m2": (ml_dtypes.float8_e5m2, 14)}[fmt]
    v = np.moveaxis(np.asarray(x, np.float32).astype(ml_dtypes.bfloat16).astype(np.float64), axis, -1)
    blocks = v.reshape(v.shape[:-1] + (-1, 32))
    amax = np.abs(blocks).max(-1, keepdims=True)
    byte = np.maximum(np.where(amax > 0, np.frexp(amax)[1] - 1 + 127, 0) - down, 1)
    scale = np.exp2(byte - 127.0)
    codes = (blocks / scale).astype(np.float32).astype(dtype).astype(np.float64)
    return np.moveaxis((codes * scale).reshape(v.shape), -1, axis)


WIDE = False


def mx_kscale(k):
    if not WIDE:
        return np.ones(k)
    levels = np.array([10, -10, 5, -5, 0])
    if k % 512:
        return np.exp2(np.random.permutation(np.resize(levels, k // 32))).repeat(32)
    a = np.empty((k // 512, 16))
    for p in range(k // 512):
        a[p, :8] = np.random.permutation(np.resize(levels, 8))
        for g in range(8):
            far = levels[np.abs(levels - a[p, g]) >= 10]
            a[p, g + 8] = far[np.random.randint(len(far))]
    return np.exp2(a.ravel()).repeat(32)


def f64(x):
    return np.asarray(x).astype(np.float64)


def striped(idx):
    return np.tile(np.asarray(idx).reshape(-1, 16).T, (8, 1)).astype(np.uint16)


def unstriped(offs):
    return offs[:16].T.reshape(-1).astype(np.int64)


E2M1 = np.array([0.0, 0.5, 1.0, 1.5, 2.0, 3.0, 4.0, 6.0, -0.0, -0.5, -1.0, -1.5, -2.0, -3.0, -4.0, -6.0])


def pack_weight(w, fmt):
    k, n = w.shape
    w = f64(np.asarray(w, np.float32).astype(ml_dtypes.bfloat16)).reshape(k // 32, 32, n)
    amax = np.abs(w).max(1)
    if fmt == "e4m3":
        byte = np.frexp(amax)[1] - 1 + 127 - 7
    else:
        mant, ex = np.frexp(amax / 6.0)
        byte = np.where(mant > 0.5, ex, ex - 1) + 127
    byte = np.clip(np.where(amax > 0, byte, 1), 1, 254)
    scaled = (w * np.exp2(127.0 - byte)[:, None, :]).reshape(k, n).astype(np.float32)
    by_word = np.ascontiguousarray(scaled.reshape(k // 512, 128, 4, n).transpose(0, 1, 3, 2))
    if fmt == "e4m3":
        words = by_word.astype(ml_dtypes.float8_e4m3fn).view(np.uint8)
    else:
        c = by_word.astype(ml_dtypes.float4_e2m1fn).view(np.uint8) & 0xF
        words = (c[..., 0::2] | (c[..., 1::2] << 4)).reshape(k // 512, 128, 2 * n)
    return np.ascontiguousarray(words), np.ascontiguousarray(byte.astype(np.uint8).reshape(k // 512, 16, n))


def unpack_weight(words, scales, fmt):
    g, _, n = scales.shape
    words = np.ascontiguousarray(words).reshape(g, 128, n, -1)
    if fmt == "e4m3":
        vals = words.view(ml_dtypes.float8_e4m3fn).astype(np.float64)
    else:
        nib = np.empty((g, 128, n, 4), np.uint8)
        nib[..., 0::2] = words & 0xF
        nib[..., 1::2] = words >> 4
        vals = E2M1[nib]
    vals = vals * np.repeat(np.exp2(scales.astype(np.float64) - 127.0), 8, axis=1)[..., None]
    return vals.transpose(0, 1, 3, 2).reshape(g * 512, n)


def bf(x):
    return np.asarray(x, np.float32).astype(ml_dtypes.bfloat16)


def planes(Y):
    r, m = Y.shape
    b = f64(bf(Y)).reshape(r // 32, 32, m)
    amax = np.abs(b).max(1)
    byte = np.clip(np.where(amax > 0, np.frexp(amax)[1] - 1 + 127 - 7, 1), 1, 254)
    codes = (b * np.exp2(127.0 - byte)[:, None, :]).reshape(r, m).astype(np.float32).astype(ml_dtypes.float8_e4m3fn).view(np.uint8)
    words = codes.reshape(r // 512, 128, 4, m).transpose(0, 1, 3, 2)
    return np.ascontiguousarray(words), np.ascontiguousarray(byte.astype(np.uint8).reshape(r // 512, 16, m))


D, T, I, Q, E, J, U = 512, 2048, 512, 256, 512, 256, 1024


def setup_inputs():
    n = np.random.standard_normal
    idx = np.random.permutation(T)[:I]
    idx2 = np.random.permutation(U)[:J]
    idx3 = np.random.permutation(Q)[:Q]
    fd = mx_kscale(D)
    fi = mx_kscale(I)
    ti = np.ones(T)
    ti[idx] = fi
    keysp = pack_weight(n((D, T)) / fd[:, None], "e2m1")
    return {
        "query": (n((D, Q)) * 0.8 / np.sqrt(D) * fd[:, None]).astype(np.float32),
        "keys_words": keysp[0],
        "keys_scales": keysp[1],
        "kept": (n((D, U)) * 1.5 / np.sqrt(D) * fd[:, None]).astype(np.float32),
        "kw1": (np.random.uniform(0.4, 1.6, (1, J))).astype(np.float32),
        "lam": (np.random.uniform(0.3, 0.7, (1, Q))).astype(np.float32),
        "width": (np.random.uniform(0.3, 0.8, (Q, 1))).astype(np.float32),
        "os": (np.random.uniform(4.0, 16.0, (1, I)) * fi).astype(np.float32),
        "vals": (n((E, T)) / ti).astype(np.float32),
        "hold": (np.random.uniform(0.3, 1.0, (1, Q))).astype(np.float32),
        "offs": striped(idx),
        "offs2": striped(idx2),
        "offs3": striped(idx3),
    }


def reference(query, keys_words, keys_scales, kept, kw1, lam, width, os, vals, hold, offs, offs2, offs3):
    idx = unstriped(offs)
    idx2 = unstriped(offs2)
    idx3 = unstriped(offs3)
    keysu = unpack_weight(keys_words, keys_scales, "e2m1")
    keysidxg = keysu[:, idx]
    queryq = mxq(f64(query), 0, "e4m3")
    a0 = keysidxg.T @ queryq
    keptidx2q = mxq(f64(kept)[:, idx2], 0, "e4m3")
    kk = keysidxg.T @ keptidx2q
    m1 = np.max(kk * f64(kw1), axis=1, keepdims=True)
    s0 = a0 - m1 * f64(lam)
    s = s0.T
    ce = (s - np.mean(s, axis=1, keepdims=True)) / f64(width)
    p = 1.0 / (np.square(ce) + 1.0)
    w = p / np.sum(p, axis=1, keepdims=True)
    wo1 = w * f64(os)
    wt1 = wo1.T
    vt1 = f64(vals)[:, idx].T
    vt1q = mxq(vt1, 0, "e4m3")
    wt1q = mxq(wt1, 0, "e4m3")
    o = vt1q.T @ wt1q
    y = o - o[:, idx3] * f64(hold)
    words, scales = planes(y)
    return y, words, scales

@@ -1,0 +1,319 @@
+from contextlib import ExitStack
+
+import concourse.mybir as mybir
+from concourse.masks import make_identity
+
+F32 = mybir.dt.float32
+BF16 = mybir.dt.bfloat16
+I32 = mybir.dt.int32
+U16 = mybir.dt.uint16
+U8 = mybir.dt.uint8
+FP8X4 = mybir.dt.float8_e4m3fn_x4
+FP4X4 = mybir.dt.float4_e2m1fn_x4
+ALU = mybir.AluOpType
+ACT = mybir.ActivationFunctionType
+AXIS_X = mybir.AxisListType.X
+
+D, T, I, Q, E, J, U = 512, 2048, 512, 256, 512, 256, 1024
+P = 128
+PACK = 4
+HALF = I // 2
+SPARE = 96
+
+FLOPS = 2 * D * I * Q + 2 * D * I * J + 2 * I * E * Q
+
+
+def interleave(engine_copy, dst, src):
+    engine_copy(
+        out=dst.rearrange("p (c i) t -> p c t i", i=4),
+        in_=src.rearrange("p t (c i) -> p c t i", i=4),
+    )
+
+
+def tile_attend_novel_typical_comparedrows_pl_kernel(
+    tc, query, keys_words, keys_scales, kept, kw1, lam, width, slot_factor, vals, hold, offs, offs2, offs3, out_0, out_1, out_2
+):
+    nc = tc.nc
+    with ExitStack() as ctx:
+        sb = ctx.enter_context(tc.tile_pool(name="sb", bufs=1))
+        ps = ctx.enter_context(tc.psum_pool(name="ps", bufs=1))
+
+        def bank(tag, name):
+            return ps.tile([P, 512], F32, tag=tag, name=name)
+
+        def quantize(src, codes, scales):
+            nc.vector.quantize_mx(out=codes.bitcast(FP8X4), scales=scales, in_=src)
+
+        offs_sb = sb.tile([P, I // 16], U16, name="offs_sb")
+        offs2_sb = sb.tile([P, J // 16], U16, name="offs2_sb")
+        offs3_sb = sb.tile([P, Q // 16], U16, name="offs3_sb")
+        key_scale_pool = sb.tile([P, T], U8, name="key_scale_pool", align_bytes=64)
+        key_word_pool = sb.tile([P, T], U16, name="key_word_pool", align_bytes=64)
+        query_raw = sb.tile([P, PACK, Q], F32, name="query_raw")
+        kept_pool = [sb.tile([P, U], F32, name="kept_pool%d" % t) for t in range(PACK)]
+        vals_pool = [sb.tile([P, T], F32, name="vals_pool%d" % t, tag="vals_pool%d" % t, align_bytes=64) for t in range(PACK)]
+        kw_cols = sb.tile([P, 2], F32, name="kw_cols")
+        os_cols = sb.tile([P, 4], F32, name="os_cols")
+        hold_cols = sb.tile([P, 2], F32, name="hold_cols")
+        lam_cols = sb.tile([P, 2], F32, name="lam_cols")
+        width_cols = sb.tile([P, 2], F32, name="width_cols")
+        kept_planes = kept.rearrange("(p t) u -> t p u", t=PACK)
+        vals_planes = vals.rearrange("(p t) n -> t p n", t=PACK)
+
+        ident = sb.tile([P, P], F32, name="ident")
+        make_identity(nc, ident[:])
+        nc.gpsimd.memset(key_scale_pool[:].bitcast(I32), 0)
+
+        nc.sync.dma_start(offs2_sb[:], offs2)
+        nc.sync.dma_start(offs_sb[:], offs)
+        with nc.allow_non_contiguous_dma(reason="one value to a partition, two columns"):
+            nc.sync.dma_start(kw_cols[:], kw1.rearrange("o (c p) -> p (o c)", p=P))
+        nc.sync.dma_start(os_cols[:], slot_factor.rearrange("o (p c) -> (o p) c", p=P))
+        nc.sync.dma_start(hold_cols[:], hold.rearrange("o (p c) -> (o p) c", p=P))
+        nc.sync.dma_start(key_word_pool[:].bitcast(I32), keys_words[0].bitcast(I32))
+        nc.sync.dma_start(kept_pool[0][:], kept_planes[0])
+        nc.sync.dma_start(kept_pool[1][:], kept_planes[1])
+        for quad in range(4):
+            nc.scalar.dma_start(
+                key_scale_pool[32 * quad : 32 * quad + 4, :].bitcast(I32),
+                keys_scales[0, 4 * quad : 4 * quad + 4, :].bitcast(I32),
+            )
+        nc.sync.dma_start(kept_pool[2][:], kept_planes[2])
+        nc.sync.dma_start(kept_pool[3][:], kept_planes[3])
+        nc.sync.dma_start(query_raw[:], query.rearrange("(p t) q -> p t q", t=PACK))
+        nc.sync.dma_start(vals_pool[0][:], vals_planes[0])
+        with nc.allow_non_contiguous_dma(reason="one value to a partition, two columns"):
+            nc.sync.dma_start(lam_cols[:], lam.rearrange("o (c p) -> p (o c)", p=P))
+            nc.sync.dma_start(width_cols[:], width.rearrange("(c p) o -> p (c o)", p=P))
+        nc.sync.dma_start(offs3_sb[:], offs3)
+        for t in range(1, PACK):
+            nc.sync.dma_start(vals_pool[t][:], vals_planes[t])
+
+        o_pool = [sb.tile([P, Q + SPARE], F32, name="o_pool%d" % t) for t in range(PACK)]
+        for t in range(PACK):
+            nc.gpsimd.memset(o_pool[t][:, Q:], 0.0)
+
+        key_words = sb.tile([P, I], U16, name="key_words", align_bytes=64)
+        nc.vector.tensor_copy(key_words[:], key_word_pool[:].indirect(offs_sb[:]))
+        key_scales = sb.tile([P, I], U8, name="key_scales", align_bytes=64)
+        nc.vector.tensor_copy(key_scales[:], key_scale_pool[:].indirect(offs_sb[:]))
+
+        kept_listed = sb.tile([P, 2, J], BF16, name="kept_listed")
+        for t in range(2):
+            nc.scalar.activation(kept_listed[:, t, :], kept_pool[t][:].indirect(offs2_sb[:]), ACT.Copy)
+        kept_bf = sb.tile([P, J, PACK], BF16, name="kept_bf", align_bytes=64)
+        interleave(nc.vector.tensor_copy, kept_bf[:, :, 0:2], kept_listed[:])
+        nc.vector.tensor_copy(kept_bf[:, :, 2], kept_pool[2][:].indirect(offs2_sb[:]))
+
+        os_row = bank("b7", "os_row")
+        for c in range(I // P):
+            nc.tensor.transpose(os_row[:, c * P : (c + 1) * P], os_cols[:, c : c + 1].to_broadcast([P, P]), ident[:])
+        hold_ps = bank("b6", "hold_ps")
+        for c in range(Q // P):
+            nc.tensor.transpose(hold_ps[:, c * P : (c + 1) * P], hold_cols[:, c : c + 1].to_broadcast([P, P]), ident[:])
+        hold_row = sb.tile([P, Q], F32, name="hold_row")
+        nc.scalar.copy(hold_row[:].rearrange("p (m c) -> p m c", c=2), hold_ps[:, 0:Q].rearrange("p (c m) -> p m c", c=2))
+
+        kept_codes = sb.tile([P, J], I32, name="kept_codes", align_bytes=64)
+        kept_scales = sb.tile([P, J], U8, name="kept_scales", align_bytes=64)
+        for c in range(2):
+            nc.vector.tensor_copy(kept_bf[:, c * P : (c + 1) * P, 3], kept_pool[3][:].indirect(offs2_sb[:, c * 8 : (c + 1) * 8]))
+        for c in range(2):
+            quantize(
+                kept_bf[:, c * P : (c + 1) * P, :].rearrange("p j t -> p (j t)"),
+                kept_codes[:, c * P : (c + 1) * P],
+                kept_scales[:, c * P : (c + 1) * P],
+            )
+        halves = [slice(h * HALF, (h + 1) * HALF) for h in range(2)]
+        kk_ps = [[bank("b%d" % (3 * c + h), "kk_ps%d%d" % (c, h)) for h in range(2)] for c in range(2)]
+        for c in range(J // P):
+            for h in range(2):
+                nc.tensor.matmul_mx(
+                    out=kk_ps[c][h][:, 0:HALF],
+                    lhsT=kept_codes[:, c * P : (c + 1) * P].bitcast(FP8X4),
+                    lhsT_scale=kept_scales[:, c * P : (c + 1) * P],
+                    rhs=key_words[:, halves[h]].bitcast(FP4X4),
+                    rhs_scale=key_scales[:, halves[h]],
+                    start=True,
+                    stop=True,
+                )
+        kk_low = [sb.tile([P, HALF], F32, name="kk_low%d" % h) for h in range(2)]
+        kk_max = [sb.tile([P, HALF], F32, name="kk_max%d" % h) for h in range(2)]
+        for h in range(2):
+            nc.scalar.activation(kk_low[h][:], kk_ps[0][h][:, 0:HALF], ACT.Copy, scale=kw_cols[:, 0:1])
+        for h in range(2):
+            nc.vector.scalar_tensor_tensor(
+                kk_max[h][:], kk_ps[1][h][:, 0:HALF], kw_cols[:, 1:2], kk_low[h][:], ALU.mult, ALU.max
+            )
+        m1 = [sb.tile([P, 2], F32, name="m1_%d" % h) for h in range(2)]
+        turned = [bank("b%d" % h, "kk_turned%d" % h) for h in range(2)]
+        for h in range(2):
+            for c in range(2):
+                nc.tensor.transpose(turned[h][:, c * P : (c + 1) * P], kk_max[h][:, c * P : (c + 1) * P], ident[:])
+        for h in range(2):
+            nc.vector.tensor_reduce(
+                m1[h][:], turned[h][:, 0:HALF].rearrange("p (c j) -> p c j", c=2), AXIS_X, ALU.max
+            )
+        m1_row = bank("b2", "m1_row")
+        for h in range(2):
+            for c in range(2):
+                col = (2 * h + c) * P
+                nc.tensor.transpose(m1_row[:, col : col + P], m1[h][:, c : c + 1].to_broadcast([P, P]), ident[:])
+
+        query_bf = sb.tile([P, Q, PACK], BF16, name="query_bf", align_bytes=64)
+        interleave(nc.vector.tensor_copy, query_bf[:], query_raw[:])
+        query_codes = sb.tile([P, Q], I32, name="query_codes", align_bytes=64)
+        query_scales = sb.tile([P, Q], U8, name="query_scales", tag="query_scales", align_bytes=64)
+        quantize(query_bf[:].rearrange("p q t -> p (q t)"), query_codes[:], query_scales[:])
+        a_ps = [bank(["b5", "b4"][c], "a_ps%d" % c) for c in range(2)]
+        for c in range(Q // P):
+            nc.tensor.matmul_mx(
+                out=a_ps[c][:],
+                lhsT=query_codes[:, c * P : (c + 1) * P].bitcast(FP8X4),
+                lhsT_scale=query_scales[:, c * P : (c + 1) * P],
+                rhs=key_words[:].bitcast(FP4X4),
+                rhs_scale=key_scales[:],
+                start=True,
+                stop=True,
+            )
+        a_sb = [sb.tile([P, I], F32, name="a_sb%d" % c, tag="a_sb%d" % c, align_bytes=64) for c in range(2)]
+        for c in range(2):
+            nc.scalar.copy(a_sb[c][:], a_ps[c][:])
+
+        vals_listed = {}
+        vals_bf = sb.tile([P, PACK, P, PACK], BF16, name="vals_bf", align_bytes=64)
+
+        def turn_pairs(src, turned_ps, dst):
+            words = src.bitcast(F32)
+            for u in range(2):
+                nc.tensor.transpose(turned_ps[:, u * P : (u + 1) * P], words[:, u : 2 * P : 2], ident[:])
+            nc.scalar.copy(
+                dst.rearrange("p c t -> p (c t)").bitcast(F32).rearrange("p (c u) -> p c u", u=2),
+                turned_ps[:, 0 : 2 * P].rearrange("p (u c) -> p c u", u=2),
+            )
+
+        def gather(on_scalar, dst, window):
+            if on_scalar:
+                nc.scalar.activation(dst, window, ACT.Copy)
+            else:
+                nc.vector.tensor_copy(dst, window)
+
+        def gather_values(t, on_scalar, tag):
+            listed = sb.tile([P, I], BF16, name="vals_listed%d" % t, tag=tag, align_bytes=64)
+            gather(on_scalar, listed[:], vals_pool[t][:].indirect(offs_sb[:]))
+            return listed
+
+        def turn_values(t):
+            turn_pairs(vals_listed[t][:], bank(["b3", "b6", "b5", "b4"][t], "vals_ps%d" % t), vals_bf[:, t])
+
+        def quantize_values(first, count, tag):
+            codes = sb.tile([P, count * P], I32, name="vals_codes%d" % first, tag=tag, align_bytes=64)
+            scales = sb.tile([P, count * P], U8, name="vals_scales%d" % first, align_bytes=64)
+            quantize(vals_bf[:, first : first + count].rearrange("p a c t -> p (a c t)"), codes[:], scales[:])
+            return [(codes[:, a * P : (a + 1) * P], scales[:, a * P : (a + 1) * P]) for a in range(count)]
+
+        def gather_values_shared(t, tag):
+            listed = sb.tile([P, I], BF16, name="vals_listed%d" % t, tag=tag, align_bytes=64)
+            for h in range(2):
+                gather(h == 1, listed[:, halves[h]], vals_pool[t][:].indirect(offs_sb[:, h * 16 : (h + 1) * 16]))
+            return listed
+
+        vals_listed.update({0: gather_values_shared(0, "query_scales")})
+
+        x = [sb.tile([P, I], F32, name="x%d" % c) for c in range(2)]
+        neg_mean = [sb.tile([P, 1], F32, name="neg_mean%d" % c) for c in range(2)]
+        for c in range(2):
+            nc.vector.scalar_tensor_tensor(
+                x[c][:], m1_row[:], lam_cols[:, c : c + 1], a_sb[c][:], ALU.mult, ALU.subtract, accum_out=neg_mean[c][:]
+            )
+        width_sq = sb.tile([P, 2], F32, name="width_sq")
+        nc.scalar.activation(width_sq[:], width_cols[:], ACT.Square, scale=float(I))
+        dist = [sb.tile([P, I], F32, name="dist%d" % c, tag=["vals_pool0", "dist1"][c], align_bytes=64) for c in range(2)]
+        root = [sb.tile([P, I], F32, name="root%d" % c, tag="root%d" % c, align_bytes=64) for c in range(2)]
+        for c in range(2):
+            nc.scalar.activation(dist[c][:], x[c][:], ACT.Square, scale=-float(I), bias=neg_mean[c][:])
+        for c in range(2):
+            nc.scalar.activation(root[c][:], dist[c][:], ACT.Abs_reciprocal_sqrt, bias=width_sq[:, c : c + 1])
+        vals_listed.update({1: gather_values(1, False, "a_sb1")})
+        part0 = sb.tile([P, I], F32, name="part0", tag="vals_pool1", align_bytes=64)
+        total = [sb.tile([P, 1], F32, name="total%d" % c) for c in range(2)]
+        nc.vector.scalar_tensor_tensor(part0[:], root[0][:], 1.0, root[0][:], ALU.mult, ALU.mult, accum_out=total[0][:])
+        vals_listed.update({2: gather_values_shared(2, "dist1")})
+        late = sb.tile([P, I + 8], F32, name="late", tag="vals_pool2", align_bytes=64)
+        part = [part0[:], late[:, 0:I]]
+        inv_total1 = sb.tile([P, 1], F32, name="inv_total1")
+        inv_total = [late[:, I : I + 1], inv_total1[:]]
+        nc.scalar.activation(part[1], root[1][:], ACT.Square, accum_out=total[1][:])
+        w_rows = [sb.tile([P, I], BF16, name="w_rows%d" % c) for c in range(2)]
+        for c in range(2):
+            nc.vector.reciprocal(inv_total[c], total[c][:])
+            nc.vector.scalar_tensor_tensor(
+                w_rows[c][:].rearrange("p (m c) -> p m c", c=4),
+                part[c].rearrange("p (m c) -> p m c", c=4),
+                inv_total[c],
+                os_row[:].rearrange("p (c m) -> p m c", c=4),
+                ALU.mult,
+                ALU.mult,
+            )
+        turn_values(0)
+        turn_values(1)
+        w_bf = sb.tile([P, 2, P, PACK], BF16, name="w_bf", align_bytes=64)
+        turn_pairs(w_rows[0][:], bank("b0", "w_ps0"), w_bf[:, 0])
+        turn_values(2)
+        turn_pairs(w_rows[1][:], bank("b1", "w_ps1"), w_bf[:, 1])
+        vals_listed.update({3: gather_values(3, False, "vals_pool2")})
+        w_codes = sb.tile([P, Q], I32, name="w_codes", tag="vals_pool3", align_bytes=64)
+        w_scales = sb.tile([P, Q], U8, name="w_scales", align_bytes=64)
+        quantize(w_bf[:].rearrange("p c q t -> p (c q t)"), w_codes[:], w_scales[:])
+        turn_values(3)
+        vals_mx = quantize_values(0, 2, "vals_pool1")
+        vals_mx.extend(quantize_values(2, 1, "vals_pool2"))
+        vals_mx.extend(quantize_values(3, 1, "vals_codes3"))
+
+        y = sb.tile([P, PACK, Q], F32, name="y")
+        out_planes = out_0.rearrange("(p t) q -> p t q", t=PACK)
+        named = {t: sb.tile([P, Q], F32, name="named%d" % t) for t in range(1, PACK)}
+        taken = [sb.tile([P, Q], F32, name="taken%d" % t) for t in range(PACK)]
+        o_tags = ["b2", "b3", "b6", "b7"]
+        for t in range(PACK):
+            o_ps = bank(o_tags[t], "o_ps%d" % t)
+            codes, scales = vals_mx[t]
+            nc.tensor.matmul_mx(
+                out=o_ps[:, 0:Q],
+                lhsT=codes.bitcast(FP8X4),
+                lhsT_scale=scales,
+                rhs=w_codes[:].bitcast(FP8X4),
+                rhs_scale=w_scales[:],
+                start=True,
+                stop=True,
+            )
+            copy_out = nc.vector.tensor_copy if t == 0 else nc.scalar.copy
+            copy_out(o_pool[t][:, 0:Q], o_ps[:, 0:Q])
+        nc.vector.tensor_tensor(taken[0][:], o_pool[0][:].indirect(offs3_sb[:]), hold_row[:], ALU.mult)
+        for t in (1, 2):
+            nc.scalar.activation(named[t][:], o_pool[t][:].indirect(offs3_sb[:]), ACT.Copy)
+        nc.scalar.activation(named[3][:, P:Q], o_pool[3][:].indirect(offs3_sb[:, 8:16]), ACT.Copy)
+        y_bf = sb.tile([P, Q, PACK], BF16, name="y_bf", align_bytes=64)
+        for t in range(PACK):
+            if t in (1, 2):
+                nc.vector.tensor_tensor(taken[t][:], named[t][:], hold_row[:], ALU.mult)
+            if t == 3:
+                nc.vector.tensor_tensor(taken[t][:, 0:P], o_pool[t][:].indirect(offs3_sb[:, 0:8]), hold_row[:, 0:P], ALU.mult)
+                nc.vector.tensor_tensor(taken[t][:, P:Q], named[t][:, P:Q], hold_row[:, P:Q], ALU.mult)
+            for cols in ([slice(0, Q)] if t < 3 else [slice(0, P), slice(P, Q)]):
+                nc.vector.tensor_tensor(y[:, t, cols], o_pool[t][:, cols], taken[t][:, cols], ALU.subtract)
+            nc.sync.dma_start(out_planes[:, t, :], y[:, t, :])
+        interleave(nc.scalar.copy, y_bf[:, :, 0:2], y[:, 0:2, :])
+        y_codes = sb.tile([P, Q], I32, name="y_codes", align_bytes=64)
+        y_scales = sb.tile([P, Q], U8, name="y_scales", align_bytes=64)
+        for cols in (slice(0, P), slice(P, Q)):
+            interleave(nc.vector.tensor_copy, y_bf[:, cols, 2:4], y[:, 2:4, cols])
+        for cols in (slice(0, P), slice(P, Q)):
+            quantize(y_bf[:, cols, :].rearrange("p q t -> p (q t)"), y_codes[:, cols], y_scales[:, cols])
+        nc.sync.dma_start(out_1[0].rearrange("p c r -> p (c r)").bitcast(I32), y_codes[:])
+        for quad in range(4):
+            queue = nc.scalar if quad % 2 == 0 else nc.sync
+            queue.dma_start(
+                out_2[0, 4 * quad : 4 * quad + 4, :].bitcast(I32),
+                y_scales[32 * quad : 32 * quad + 4, :].bitcast(I32),
+            )

@@ -63,6 +63,10 @@ def tile_attend_novel_typical_comparedrows_pl_kernel(
         ident = sb.tile([P, P], F32, name="ident")
         make_identity(nc, ident[:])
         nc.gpsimd.memset(key_scale_pool[:].bitcast(I32), 0)
+        warm_in = sb.tile([P, 1], F32, name="warm_in")
+        warm_out = sb.tile([P, 1], F32, name="warm_out")
+        nc.vector.memset(warm_in[:], 1.0)
+        nc.scalar.activation(warm_out[:], warm_in[:], ACT.Abs_reciprocal_sqrt)
 
         nc.sync.dma_start(offs2_sb[:], offs2)
         nc.sync.dma_start(offs_sb[:], offs)

@@ -208,7 +208,7 @@ def tile_attend_novel_typical_comparedrows_pl_kernel(
             return listed
 
         def turn_values(t):
-            turn_pairs(vals_listed[t][:], bank(["b3", "b6", "b5", "b4"][t], "vals_ps%d" % t), vals_bf[:, t])
+            turn_pairs(vals_listed[t][:], bank(["b3", "b1", "b5", "b4"][t], "vals_ps%d" % t), vals_bf[:, t])
 
         def quantize_values(first, count, tag):
             codes = sb.tile([P, count * P], I32, name="vals_codes%d" % first, tag=tag, align_bytes=64)
@@ -239,22 +239,19 @@ def tile_attend_novel_typical_comparedrows_pl_kernel(
         for c in range(2):
             nc.scalar.activation(root[c][:], dist[c][:], ACT.Abs_reciprocal_sqrt, bias=width_sq[:, c : c + 1])
         vals_listed.update({1: gather_values(1, False, "a_sb1")})
-        part0 = sb.tile([P, I], F32, name="part0", tag="vals_pool1", align_bytes=64)
+        vals_listed.update({2: gather_values(2, False, "vals_listed2")})
+        part = [sb.tile([P, I], F32, name="part%d" % c, tag="part%d" % c, align_bytes=64) for c in range(2)]
         total = [sb.tile([P, 1], F32, name="total%d" % c) for c in range(2)]
-        nc.vector.scalar_tensor_tensor(part0[:], root[0][:], 1.0, root[0][:], ALU.mult, ALU.mult, accum_out=total[0][:])
-        vals_listed.update({2: gather_values_shared(2, "dist1")})
-        late = sb.tile([P, I + 8], F32, name="late", tag="vals_pool2", align_bytes=64)
-        part = [part0[:], late[:, 0:I]]
-        inv_total1 = sb.tile([P, 1], F32, name="inv_total1")
-        inv_total = [late[:, I : I + 1], inv_total1[:]]
-        nc.scalar.activation(part[1], root[1][:], ACT.Square, accum_out=total[1][:])
+        for c in range(2):
+            nc.scalar.activation(part[c][:], root[c][:], ACT.Square, accum_out=total[c][:])
+        inv_total = sb.tile([P, 2], F32, name="inv_total", tag="vals_pool2", align_bytes=64)
         w_rows = [sb.tile([P, I], BF16, name="w_rows%d" % c) for c in range(2)]
         for c in range(2):
-            nc.vector.reciprocal(inv_total[c], total[c][:])
+            nc.vector.reciprocal(inv_total[:, c : c + 1], total[c][:])
             nc.vector.scalar_tensor_tensor(
                 w_rows[c][:].rearrange("p (m c) -> p m c", c=4),
-                part[c].rearrange("p (m c) -> p m c", c=4),
-                inv_total[c],
+                part[c][:].rearrange("p (m c) -> p m c", c=4),
+                inv_total[:, c : c + 1],
                 os_row[:].rearrange("p (c m) -> p m c", c=4),
                 ALU.mult,
                 ALU.mult,
@@ -265,25 +262,26 @@ def tile_attend_novel_typical_comparedrows_pl_kernel(
         turn_pairs(w_rows[0][:], bank("b0", "w_ps0"), w_bf[:, 0])
         turn_values(2)
         turn_pairs(w_rows[1][:], bank("b1", "w_ps1"), w_bf[:, 1])
-        vals_listed.update({3: gather_values(3, False, "vals_pool2")})
+        vals_listed.update({3: gather_values(3, False, "part1")})
         w_codes = sb.tile([P, Q], I32, name="w_codes", tag="vals_pool3", align_bytes=64)
         w_scales = sb.tile([P, Q], U8, name="w_scales", align_bytes=64)
         quantize(w_bf[:].rearrange("p c q t -> p (c q t)"), w_codes[:], w_scales[:])
         turn_values(3)
-        vals_mx = quantize_values(0, 2, "vals_pool1")
-        vals_mx.extend(quantize_values(2, 1, "vals_pool2"))
+        vals_mx = quantize_values(0, 2, "part0")
+        vals_mx.extend(quantize_values(2, 1, "part1"))
         vals_mx.extend(quantize_values(3, 1, "vals_codes3"))
 
         y = sb.tile([P, PACK, Q], F32, name="y")
         out_planes = out_0.rearrange("(p t) q -> p t q", t=PACK)
         named = {t: sb.tile([P, Q], F32, name="named%d" % t) for t in range(1, PACK)}
         taken = [sb.tile([P, Q], F32, name="taken%d" % t) for t in range(PACK)]
-        o_tags = ["b2", "b3", "b6", "b7"]
+        o_tags = ["b2", "b3", "b0", "b7"]
+        o_ps = []
         for t in range(PACK):
-            o_ps = bank(o_tags[t], "o_ps%d" % t)
+            o_ps.append(bank(o_tags[t], "o_ps%d" % t))
             codes, scales = vals_mx[t]
             nc.tensor.matmul_mx(
-                out=o_ps[:, 0:Q],
+                out=o_ps[t][:, 0:Q],
                 lhsT=codes.bitcast(FP8X4),
                 lhsT_scale=scales,
                 rhs=w_codes[:].bitcast(FP8X4),
@@ -292,7 +290,7 @@ def tile_attend_novel_typical_comparedrows_pl_kernel(
                 stop=True,
             )
             copy_out = nc.vector.tensor_copy if t == 0 else nc.scalar.copy
-            copy_out(o_pool[t][:, 0:Q], o_ps[:, 0:Q])
+            copy_out(o_pool[t][:, 0:Q], o_ps[t][:, 0:Q])
         nc.vector.tensor_tensor(taken[0][:], o_pool[0][:].indirect(offs3_sb[:]), hold_row[:], ALU.mult)
         for t in (1, 2):
             nc.scalar.activation(named[t][:], o_pool[t][:].indirect(offs3_sb[:]), ACT.Copy)
@@ -300,12 +298,20 @@ def tile_attend_novel_typical_comparedrows_pl_kernel(
         y_bf = sb.tile([P, Q, PACK], BF16, name="y_bf", align_bytes=64)
         for t in range(PACK):
             if t in (1, 2):
-                nc.vector.tensor_tensor(taken[t][:], named[t][:], hold_row[:], ALU.mult)
+                nc.vector.tensor_tensor(
+                    taken[t][:].rearrange("p (m c) -> p m c", c=2),
+                    named[t][:].rearrange("p (m c) -> p m c", c=2),
+                    hold_ps[:, 0:Q].rearrange("p (c m) -> p m c", c=2),
+                    ALU.mult,
+                )
             if t == 3:
                 nc.vector.tensor_tensor(taken[t][:, 0:P], o_pool[t][:].indirect(offs3_sb[:, 0:8]), hold_row[:, 0:P], ALU.mult)
                 nc.vector.tensor_tensor(taken[t][:, P:Q], named[t][:, P:Q], hold_row[:, P:Q], ALU.mult)
-            for cols in ([slice(0, Q)] if t < 3 else [slice(0, P), slice(P, Q)]):
-                nc.vector.tensor_tensor(y[:, t, cols], o_pool[t][:, cols], taken[t][:, cols], ALU.subtract)
+            if t < 2:
+                nc.gpsimd.tensor_tensor(y[:, t, :], o_pool[t][:, 0:Q], taken[t][:], ALU.subtract)
+            else:
+                for cols in ([slice(0, Q)] if t < 3 else [slice(0, P), slice(P, Q)]):
+                    nc.vector.tensor_tensor(y[:, t, cols], o_ps[t][:, cols], taken[t][:, cols], ALU.subtract)
             nc.sync.dma_start(out_planes[:, t, :], y[:, t, :])
         interleave(nc.scalar.copy, y_bf[:, :, 0:2], y[:, 0:2, :])
         y_codes = sb.tile([P, Q], I32, name="y_codes", align_bytes=64)

@@ -30,6 +30,13 @@ def interleave(engine_copy, dst, src):
     )
 
 
+def interleave_dealt(engine_copy, dst, src):
+    engine_copy(
+        out=dst.rearrange("p (c a b) t -> p a t b c", c=2, b=2),
+        in_=src.rearrange("p t (a b c) -> p a t b c", c=2, b=2),
+    )
+
+
 def tile_attend_novel_typical_comparedrows_pl_kernel(
     tc, query, keys_words, keys_scales, kept, kw1, lam, width, slot_factor, vals, hold, offs, offs2, offs3, out_0, out_1, out_2
 ):
@@ -70,8 +77,7 @@ def tile_attend_novel_typical_comparedrows_pl_kernel(
 
         nc.sync.dma_start(offs2_sb[:], offs2)
         nc.sync.dma_start(offs_sb[:], offs)
-        with nc.allow_non_contiguous_dma(reason="one value to a partition, two columns"):
-            nc.sync.dma_start(kw_cols[:], kw1.rearrange("o (c p) -> p (o c)", p=P))
+        nc.sync.dma_start(kw_cols[:], kw1.rearrange("o (p c) -> (o p) c", p=P))
         nc.sync.dma_start(os_cols[:], slot_factor.rearrange("o (p c) -> (o p) c", p=P))
         nc.sync.dma_start(hold_cols[:], hold.rearrange("o (p c) -> (o p) c", p=P))
         nc.sync.dma_start(key_word_pool[:].bitcast(I32), keys_words[0].bitcast(I32))
@@ -86,9 +92,8 @@ def tile_attend_novel_typical_comparedrows_pl_kernel(
         nc.sync.dma_start(kept_pool[3][:], kept_planes[3])
         nc.sync.dma_start(query_raw[:], query.rearrange("(p t) q -> p t q", t=PACK))
         nc.sync.dma_start(vals_pool[0][:], vals_planes[0])
-        with nc.allow_non_contiguous_dma(reason="one value to a partition, two columns"):
-            nc.sync.dma_start(lam_cols[:], lam.rearrange("o (c p) -> p (o c)", p=P))
-            nc.sync.dma_start(width_cols[:], width.rearrange("(c p) o -> p (c o)", p=P))
+        nc.sync.dma_start(lam_cols[:], lam.rearrange("o (p c) -> (o p) c", p=P))
+        nc.sync.dma_start(width_cols[:], width.rearrange("(p c) o -> p (c o)", p=P))
         nc.sync.dma_start(offs3_sb[:], offs3)
         for t in range(1, PACK):
             nc.sync.dma_start(vals_pool[t][:], vals_planes[t])
@@ -106,8 +111,9 @@ def tile_attend_novel_typical_comparedrows_pl_kernel(
         for t in range(2):
             nc.scalar.activation(kept_listed[:, t, :], kept_pool[t][:].indirect(offs2_sb[:]), ACT.Copy)
         kept_bf = sb.tile([P, J, PACK], BF16, name="kept_bf", align_bytes=64)
-        interleave(nc.vector.tensor_copy, kept_bf[:, :, 0:2], kept_listed[:])
-        nc.vector.tensor_copy(kept_bf[:, :, 2], kept_pool[2][:].indirect(offs2_sb[:]))
+        interleave_dealt(nc.vector.tensor_copy, kept_bf[:, :, 0:2], kept_listed[:])
+        kept_dealt = kept_bf[:].rearrange("p (c m) t -> p m c t", c=2)
+        nc.vector.tensor_copy(kept_dealt[:, :, :, 2], kept_pool[2][:].indirect(offs2_sb[:]))
 
         os_row = bank("b7", "os_row")
         for c in range(I // P):
@@ -120,8 +126,7 @@ def tile_attend_novel_typical_comparedrows_pl_kernel(
 
         kept_codes = sb.tile([P, J], I32, name="kept_codes", align_bytes=64)
         kept_scales = sb.tile([P, J], U8, name="kept_scales", align_bytes=64)
-        for c in range(2):
-            nc.vector.tensor_copy(kept_bf[:, c * P : (c + 1) * P, 3], kept_pool[3][:].indirect(offs2_sb[:, c * 8 : (c + 1) * 8]))
+        nc.vector.tensor_copy(kept_dealt[:, :, :, 3], kept_pool[3][:].indirect(offs2_sb[:]))
         for c in range(2):
             quantize(
                 kept_bf[:, c * P : (c + 1) * P, :].rearrange("p j t -> p (j t)"),
@@ -165,7 +170,7 @@ def tile_attend_novel_typical_comparedrows_pl_kernel(
                 nc.tensor.transpose(m1_row[:, col : col + P], m1[h][:, c : c + 1].to_broadcast([P, P]), ident[:])
 
         query_bf = sb.tile([P, Q, PACK], BF16, name="query_bf", align_bytes=64)
-        interleave(nc.vector.tensor_copy, query_bf[:], query_raw[:])
+        interleave_dealt(nc.vector.tensor_copy, query_bf[:], query_raw[:])
         query_codes = sb.tile([P, Q], I32, name="query_codes", align_bytes=64)
         query_scales = sb.tile([P, Q], U8, name="query_scales", tag="query_scales", align_bytes=64)
         quantize(query_bf[:].rearrange("p q t -> p (q t)"), query_codes[:], query_scales[:])
@@ -290,7 +295,10 @@ def tile_attend_novel_typical_comparedrows_pl_kernel(
                 stop=True,
             )
             copy_out = nc.vector.tensor_copy if t == 0 else nc.scalar.copy
-            copy_out(o_pool[t][:, 0:Q], o_ps[t][:, 0:Q])
+            copy_out(
+                o_pool[t][:, 0:Q].rearrange("p (m c) -> p m c", c=2),
+                o_ps[t][:, 0:Q].rearrange("p (c m) -> p m c", c=2),
+            )
         nc.vector.tensor_tensor(taken[0][:], o_pool[0][:].indirect(offs3_sb[:]), hold_row[:], ALU.mult)
         for t in (1, 2):
             nc.scalar.activation(named[t][:], o_pool[t][:].indirect(offs3_sb[:]), ACT.Copy)
@@ -310,8 +318,13 @@ def tile_attend_novel_typical_comparedrows_pl_kernel(
             if t < 2:
                 nc.gpsimd.tensor_tensor(y[:, t, :], o_pool[t][:, 0:Q], taken[t][:], ALU.subtract)
             else:
-                for cols in ([slice(0, Q)] if t < 3 else [slice(0, P), slice(P, Q)]):
-                    nc.vector.tensor_tensor(y[:, t, cols], o_ps[t][:, cols], taken[t][:, cols], ALU.subtract)
+                for ms in ([slice(0, P)] if t < 3 else [slice(0, P // 2), slice(P // 2, P)]):
+                    nc.vector.tensor_tensor(
+                        y[:, t, :].rearrange("p (m c) -> p m c", c=2)[:, ms, :],
+                        o_ps[t][:, 0:Q].rearrange("p (c m) -> p m c", c=2)[:, ms, :],
+                        taken[t][:].rearrange("p (m c) -> p m c", c=2)[:, ms, :],
+                        ALU.subtract,
+                    )
             nc.sync.dma_start(out_planes[:, t, :], y[:, t, :])
         interleave(nc.scalar.copy, y_bf[:, :, 0:2], y[:, 0:2, :])
         y_codes = sb.tile([P, Q], I32, name="y_codes", align_bytes=64)

from contextlib import ExitStack

import concourse.mybir as mybir
from concourse.masks import make_identity

F32 = mybir.dt.float32
BF16 = mybir.dt.bfloat16
I32 = mybir.dt.int32
U16 = mybir.dt.uint16
U8 = mybir.dt.uint8
FP8X4 = mybir.dt.float8_e4m3fn_x4
FP4X4 = mybir.dt.float4_e2m1fn_x4
ALU = mybir.AluOpType
ACT = mybir.ActivationFunctionType
AXIS_X = mybir.AxisListType.X

D, T, I, Q, E, J, U = 512, 2048, 512, 256, 512, 256, 1024
P = 128
PACK = 4
HALF = I // 2
SPARE = 96

FLOPS = 2 * D * I * Q + 2 * D * I * J + 2 * I * E * Q


def interleave(engine_copy, dst, src):
    engine_copy(
        out=dst.rearrange("p (c i) t -> p c t i", i=4),
        in_=src.rearrange("p t (c i) -> p c t i", i=4),
    )


def interleave_dealt(engine_copy, dst, src):
    engine_copy(
        out=dst.rearrange("p (c a b) t -> p a t b c", c=2, b=2),
        in_=src.rearrange("p t (a b c) -> p a t b c", c=2, b=2),
    )


def tile_attend_novel_typical_comparedrows_pl_kernel(
    tc, query, keys_words, keys_scales, kept, kw1, lam, width, slot_factor, vals, hold, offs, offs2, offs3, out_0, out_1, out_2
):
    nc = tc.nc
    with ExitStack() as ctx:
        sb = ctx.enter_context(tc.tile_pool(name="sb", bufs=1))
        ps = ctx.enter_context(tc.psum_pool(name="ps", bufs=1))

        def bank(tag, name):
            return ps.tile([P, 512], F32, tag=tag, name=name)

        def quantize(src, codes, scales):
            nc.vector.quantize_mx(out=codes.bitcast(FP8X4), scales=scales, in_=src)

        offs_sb = sb.tile([P, I // 16], U16, name="offs_sb")
        offs2_sb = sb.tile([P, J // 16], U16, name="offs2_sb")
        offs3_sb = sb.tile([P, Q // 16], U16, name="offs3_sb")
        key_scale_pool = sb.tile([P, T], U8, name="key_scale_pool", align_bytes=64)
        key_word_pool = sb.tile([P, T], U16, name="key_word_pool", align_bytes=64)
        query_raw = sb.tile([P, PACK, Q], F32, name="query_raw")
        kept_pool = [sb.tile([P, U], F32, name="kept_pool%d" % t) for t in range(PACK)]
        vals_pool = [sb.tile([P, T], F32, name="vals_pool%d" % t, tag="vals_pool%d" % t, align_bytes=64) for t in range(PACK)]
        kw_cols = sb.tile([P, 2], F32, name="kw_cols")
        os_cols = sb.tile([P, 4], F32, name="os_cols")
        hold_cols = sb.tile([P, 2], F32, name="hold_cols")
        lam_cols = sb.tile([P, 2], F32, name="lam_cols")
        width_cols = sb.tile([P, 2], F32, name="width_cols")
        kept_planes = kept.rearrange("(p t) u -> t p u", t=PACK)
        vals_planes = vals.rearrange("(p t) n -> t p n", t=PACK)

        ident = sb.tile([P, P], F32, name="ident")
        make_identity(nc, ident[:])
        nc.gpsimd.memset(key_scale_pool[:].bitcast(I32), 0)
        warm_in = sb.tile([P, 1], F32, name="warm_in")
        warm_out = sb.tile([P, 1], F32, name="warm_out")
        nc.vector.memset(warm_in[:], 1.0)
        nc.scalar.activation(warm_out[:], warm_in[:], ACT.Abs_reciprocal_sqrt)

        nc.sync.dma_start(offs2_sb[:], offs2)
        nc.sync.dma_start(offs_sb[:], offs)
        nc.sync.dma_start(kw_cols[:], kw1.rearrange("o (p c) -> (o p) c", p=P))
        nc.sync.dma_start(os_cols[:], slot_factor.rearrange("o (p c) -> (o p) c", p=P))
        nc.sync.dma_start(hold_cols[:], hold.rearrange("o (p c) -> (o p) c", p=P))
        nc.sync.dma_start(key_word_pool[:].bitcast(I32), keys_words[0].bitcast(I32))
        nc.sync.dma_start(kept_pool[0][:], kept_planes[0])
        nc.sync.dma_start(kept_pool[1][:], kept_planes[1])
        for quad in range(4):
            nc.scalar.dma_start(
                key_scale_pool[32 * quad : 32 * quad + 4, :].bitcast(I32),
                keys_scales[0, 4 * quad : 4 * quad + 4, :].bitcast(I32),
            )
        nc.sync.dma_start(kept_pool[2][:], kept_planes[2])
        nc.sync.dma_start(kept_pool[3][:], kept_planes[3])
        nc.sync.dma_start(query_raw[:], query.rearrange("(p t) q -> p t q", t=PACK))
        nc.sync.dma_start(vals_pool[0][:], vals_planes[0])
        nc.sync.dma_start(lam_cols[:], lam.rearrange("o (p c) -> (o p) c", p=P))
        nc.sync.dma_start(width_cols[:], width.rearrange("(p c) o -> p (c o)", p=P))
        nc.sync.dma_start(offs3_sb[:], offs3)
        for t in range(1, PACK):
            nc.sync.dma_start(vals_pool[t][:], vals_planes[t])

        o_pool = [sb.tile([P, Q + SPARE], F32, name="o_pool%d" % t) for t in range(PACK)]
        for t in range(PACK):
            nc.gpsimd.memset(o_pool[t][:, Q:], 0.0)

        key_words = sb.tile([P, I], U16, name="key_words", align_bytes=64)
        nc.vector.tensor_copy(key_words[:], key_word_pool[:].indirect(offs_sb[:]))
        key_scales = sb.tile([P, I], U8, name="key_scales", align_bytes=64)
        nc.vector.tensor_copy(key_scales[:], key_scale_pool[:].indirect(offs_sb[:]))

        kept_listed = sb.tile([P, 2, J], BF16, name="kept_listed")
        for t in range(2):
            nc.scalar.activation(kept_listed[:, t, :], kept_pool[t][:].indirect(offs2_sb[:]), ACT.Copy)
        kept_bf = sb.tile([P, J, PACK], BF16, name="kept_bf", align_bytes=64)
        interleave_dealt(nc.vector.tensor_copy, kept_bf[:, :, 0:2], kept_listed[:])
        kept_dealt = kept_bf[:].rearrange("p (c m) t -> p m c t", c=2)
        nc.vector.tensor_copy(kept_dealt[:, :, :, 2], kept_pool[2][:].indirect(offs2_sb[:]))

        os_row = bank("b7", "os_row")
        for c in range(I // P):
            nc.tensor.transpose(os_row[:, c * P : (c + 1) * P], os_cols[:, c : c + 1].to_broadcast([P, P]), ident[:])
        hold_ps = bank("b6", "hold_ps")
        for c in range(Q // P):
            nc.tensor.transpose(hold_ps[:, c * P : (c + 1) * P], hold_cols[:, c : c + 1].to_broadcast([P, P]), ident[:])
        hold_row = sb.tile([P, Q], F32, name="hold_row")
        nc.scalar.copy(hold_row[:].rearrange("p (m c) -> p m c", c=2), hold_ps[:, 0:Q].rearrange("p (c m) -> p m c", c=2))

        kept_codes = sb.tile([P, J], I32, name="kept_codes", align_bytes=64)
        kept_scales = sb.tile([P, J], U8, name="kept_scales", align_bytes=64)
        nc.vector.tensor_copy(kept_dealt[:, :, :, 3], kept_pool[3][:].indirect(offs2_sb[:]))
        for c in range(2):
            quantize(
                kept_bf[:, c * P : (c + 1) * P, :].rearrange("p j t -> p (j t)"),
                kept_codes[:, c * P : (c + 1) * P],
                kept_scales[:, c * P : (c + 1) * P],
            )
        halves = [slice(h * HALF, (h + 1) * HALF) for h in range(2)]
        kk_ps = [[bank("b%d" % (3 * c + h), "kk_ps%d%d" % (c, h)) for h in range(2)] for c in range(2)]
        for c in range(J // P):
            for h in range(2):
                nc.tensor.matmul_mx(
                    out=kk_ps[c][h][:, 0:HALF],
                    lhsT=kept_codes[:, c * P : (c + 1) * P].bitcast(FP8X4),
                    lhsT_scale=kept_scales[:, c * P : (c + 1) * P],
                    rhs=key_words[:, halves[h]].bitcast(FP4X4),
                    rhs_scale=key_scales[:, halves[h]],
                    start=True,
                    stop=True,
                )
        kk_low = [sb.tile([P, HALF], F32, name="kk_low%d" % h) for h in range(2)]
        kk_max = [sb.tile([P, HALF], F32, name="kk_max%d" % h) for h in range(2)]
        for h in range(2):
            nc.scalar.activation(kk_low[h][:], kk_ps[0][h][:, 0:HALF], ACT.Copy, scale=kw_cols[:, 0:1])
        for h in range(2):
            nc.vector.scalar_tensor_tensor(
                kk_max[h][:], kk_ps[1][h][:, 0:HALF], kw_cols[:, 1:2], kk_low[h][:], ALU.mult, ALU.max
            )
        m1 = [sb.tile([P, 2], F32, name="m1_%d" % h) for h in range(2)]
        turned = [bank("b%d" % h, "kk_turned%d" % h) for h in range(2)]
        for h in range(2):
            for c in range(2):
                nc.tensor.transpose(turned[h][:, c * P : (c + 1) * P], kk_max[h][:, c * P : (c + 1) * P], ident[:])
        for h in range(2):
            nc.vector.tensor_reduce(
                m1[h][:], turned[h][:, 0:HALF].rearrange("p (c j) -> p c j", c=2), AXIS_X, ALU.max
            )
        m1_row = bank("b2", "m1_row")
        for h in range(2):
            for c in range(2):
                col = (2 * h + c) * P
                nc.tensor.transpose(m1_row[:, col : col + P], m1[h][:, c : c + 1].to_broadcast([P, P]), ident[:])

        query_bf = sb.tile([P, Q, PACK], BF16, name="query_bf", align_bytes=64)
        interleave_dealt(nc.vector.tensor_copy, query_bf[:], query_raw[:])
        query_codes = sb.tile([P, Q], I32, name="query_codes", align_bytes=64)
        query_scales = sb.tile([P, Q], U8, name="query_scales", tag="query_scales", align_bytes=64)
        quantize(query_bf[:].rearrange("p q t -> p (q t)"), query_codes[:], query_scales[:])
        a_ps = [bank(["b5", "b4"][c], "a_ps%d" % c) for c in range(2)]
        for c in range(Q // P):
            nc.tensor.matmul_mx(
                out=a_ps[c][:],
                lhsT=query_codes[:, c * P : (c + 1) * P].bitcast(FP8X4),
                lhsT_scale=query_scales[:, c * P : (c + 1) * P],
                rhs=key_words[:].bitcast(FP4X4),
                rhs_scale=key_scales[:],
                start=True,
                stop=True,
            )
        a_sb = [sb.tile([P, I], F32, name="a_sb%d" % c, tag="a_sb%d" % c, align_bytes=64) for c in range(2)]
        for c in range(2):
            nc.scalar.copy(a_sb[c][:], a_ps[c][:])

        vals_listed = {}
        vals_bf = sb.tile([P, PACK, P, PACK], BF16, name="vals_bf", align_bytes=64)

        def turn_pairs(src, turned_ps, dst):
            words = src.bitcast(F32)
            for u in range(2):
                nc.tensor.transpose(turned_ps[:, u * P : (u + 1) * P], words[:, u : 2 * P : 2], ident[:])
            nc.scalar.copy(
                dst.rearrange("p c t -> p (c t)").bitcast(F32).rearrange("p (c u) -> p c u", u=2),
                turned_ps[:, 0 : 2 * P].rearrange("p (u c) -> p c u", u=2),
            )

        def gather(on_scalar, dst, window):
            if on_scalar:
                nc.scalar.activation(dst, window, ACT.Copy)
            else:
                nc.vector.tensor_copy(dst, window)

        def gather_values(t, on_scalar, tag):
            listed = sb.tile([P, I], BF16, name="vals_listed%d" % t, tag=tag, align_bytes=64)
            gather(on_scalar, listed[:], vals_pool[t][:].indirect(offs_sb[:]))
            return listed

        def turn_values(t):
            turn_pairs(vals_listed[t][:], bank(["b3", "b1", "b5", "b4"][t], "vals_ps%d" % t), vals_bf[:, t])

        def quantize_values(first, count, tag):
            codes = sb.tile([P, count * P], I32, name="vals_codes%d" % first, tag=tag, align_bytes=64)
            scales = sb.tile([P, count * P], U8, name="vals_scales%d" % first, align_bytes=64)
            quantize(vals_bf[:, first : first + count].rearrange("p a c t -> p (a c t)"), codes[:], scales[:])
            return [(codes[:, a * P : (a + 1) * P], scales[:, a * P : (a + 1) * P]) for a in range(count)]

        def gather_values_shared(t, tag):
            listed = sb.tile([P, I], BF16, name="vals_listed%d" % t, tag=tag, align_bytes=64)
            for h in range(2):
                gather(h == 1, listed[:, halves[h]], vals_pool[t][:].indirect(offs_sb[:, h * 16 : (h + 1) * 16]))
            return listed

        vals_listed.update({0: gather_values_shared(0, "query_scales")})

        x = [sb.tile([P, I], F32, name="x%d" % c) for c in range(2)]
        neg_mean = [sb.tile([P, 1], F32, name="neg_mean%d" % c) for c in range(2)]
        for c in range(2):
            nc.vector.scalar_tensor_tensor(
                x[c][:], m1_row[:], lam_cols[:, c : c + 1], a_sb[c][:], ALU.mult, ALU.subtract, accum_out=neg_mean[c][:]
            )
        width_sq = sb.tile([P, 2], F32, name="width_sq")
        nc.scalar.activation(width_sq[:], width_cols[:], ACT.Square, scale=float(I))
        dist = [sb.tile([P, I], F32, name="dist%d" % c, tag=["vals_pool0", "dist1"][c], align_bytes=64) for c in range(2)]
        root = [sb.tile([P, I], F32, name="root%d" % c, tag="root%d" % c, align_bytes=64) for c in range(2)]
        for c in range(2):
            nc.scalar.activation(dist[c][:], x[c][:], ACT.Square, scale=-float(I), bias=neg_mean[c][:])
        for c in range(2):
            nc.scalar.activation(root[c][:], dist[c][:], ACT.Abs_reciprocal_sqrt, bias=width_sq[:, c : c + 1])
        vals_listed.update({1: gather_values(1, False, "a_sb1")})
        vals_listed.update({2: gather_values(2, False, "vals_listed2")})
        part = [sb.tile([P, I], F32, name="part%d" % c, tag="part%d" % c, align_bytes=64) for c in range(2)]
        total = [sb.tile([P, 1], F32, name="total%d" % c) for c in range(2)]
        for c in range(2):
            nc.scalar.activation(part[c][:], root[c][:], ACT.Square, accum_out=total[c][:])
        inv_total = sb.tile([P, 2], F32, name="inv_total", tag="vals_pool2", align_bytes=64)
        w_rows = [sb.tile([P, I], BF16, name="w_rows%d" % c) for c in range(2)]
        for c in range(2):
            nc.vector.reciprocal(inv_total[:, c : c + 1], total[c][:])
            nc.vector.scalar_tensor_tensor(
                w_rows[c][:].rearrange("p (m c) -> p m c", c=4),
                part[c][:].rearrange("p (m c) -> p m c", c=4),
                inv_total[:, c : c + 1],
                os_row[:].rearrange("p (c m) -> p m c", c=4),
                ALU.mult,
                ALU.mult,
            )
        turn_values(0)
        turn_values(1)
        w_bf = sb.tile([P, 2, P, PACK], BF16, name="w_bf", align_bytes=64)
        turn_pairs(w_rows[0][:], bank("b0", "w_ps0"), w_bf[:, 0])
        turn_values(2)
        turn_pairs(w_rows[1][:], bank("b1", "w_ps1"), w_bf[:, 1])
        vals_listed.update({3: gather_values(3, False, "part1")})
        w_codes = sb.tile([P, Q], I32, name="w_codes", tag="vals_pool3", align_bytes=64)
        w_scales = sb.tile([P, Q], U8, name="w_scales", align_bytes=64)
        quantize(w_bf[:].rearrange("p c q t -> p (c q t)"), w_codes[:], w_scales[:])
        turn_values(3)
        vals_mx = quantize_values(0, 2, "part0")
        vals_mx.extend(quantize_values(2, 1, "part1"))
        vals_mx.extend(quantize_values(3, 1, "vals_codes3"))

        y = sb.tile([P, PACK, Q], F32, name="y")
        out_planes = out_0.rearrange("(p t) q -> p t q", t=PACK)
        named = {t: sb.tile([P, Q], F32, name="named%d" % t) for t in range(1, PACK)}
        taken = [sb.tile([P, Q], F32, name="taken%d" % t) for t in range(PACK)]
        o_tags = ["b2", "b3", "b0", "b7"]
        o_ps = []
        for t in range(PACK):
            o_ps.append(bank(o_tags[t], "o_ps%d" % t))
            codes, scales = vals_mx[t]
            nc.tensor.matmul_mx(
                out=o_ps[t][:, 0:Q],
                lhsT=codes.bitcast(FP8X4),
                lhsT_scale=scales,
                rhs=w_codes[:].bitcast(FP8X4),
                rhs_scale=w_scales[:],
                start=True,
                stop=True,
            )
            copy_out = nc.vector.tensor_copy if t == 0 else nc.scalar.copy
            copy_out(
                o_pool[t][:, 0:Q].rearrange("p (m c) -> p m c", c=2),
                o_ps[t][:, 0:Q].rearrange("p (c m) -> p m c", c=2),
            )
        nc.vector.tensor_tensor(taken[0][:], o_pool[0][:].indirect(offs3_sb[:]), hold_row[:], ALU.mult)
        for t in (1, 2):
            nc.scalar.activation(named[t][:], o_pool[t][:].indirect(offs3_sb[:]), ACT.Copy)
        nc.scalar.activation(named[3][:, P:Q], o_pool[3][:].indirect(offs3_sb[:, 8:16]), ACT.Copy)
        y_bf = sb.tile([P, Q, PACK], BF16, name="y_bf", align_bytes=64)
        for t in range(PACK):
            if t in (1, 2):
                nc.vector.tensor_tensor(
                    taken[t][:].rearrange("p (m c) -> p m c", c=2),
                    named[t][:].rearrange("p (m c) -> p m c", c=2),
                    hold_ps[:, 0:Q].rearrange("p (c m) -> p m c", c=2),
                    ALU.mult,
                )
            if t == 3:
                nc.vector.tensor_tensor(taken[t][:, 0:P], o_pool[t][:].indirect(offs3_sb[:, 0:8]), hold_row[:, 0:P], ALU.mult)
                nc.vector.tensor_tensor(taken[t][:, P:Q], named[t][:, P:Q], hold_row[:, P:Q], ALU.mult)
            if t < 2:
                nc.gpsimd.tensor_tensor(y[:, t, :], o_pool[t][:, 0:Q], taken[t][:], ALU.subtract)
            else:
                for ms in ([slice(0, P)] if t < 3 else [slice(0, P // 2), slice(P // 2, P)]):
                    nc.vector.tensor_tensor(
                        y[:, t, :].rearrange("p (m c) -> p m c", c=2)[:, ms, :],
                        o_ps[t][:, 0:Q].rearrange("p (c m) -> p m c", c=2)[:, ms, :],
                        taken[t][:].rearrange("p (m c) -> p m c", c=2)[:, ms, :],
                        ALU.subtract,
                    )
            nc.sync.dma_start(out_planes[:, t, :], y[:, t, :])
        interleave(nc.scalar.copy, y_bf[:, :, 0:2], y[:, 0:2, :])
        y_codes = sb.tile([P, Q], I32, name="y_codes", align_bytes=64)
        y_scales = sb.tile([P, Q], U8, name="y_scales", align_bytes=64)
        for cols in (slice(0, P), slice(P, Q)):
            interleave(nc.vector.tensor_copy, y_bf[:, cols, 2:4], y[:, 2:4, cols])
        for cols in (slice(0, P), slice(P, Q)):
            quantize(y_bf[:, cols, :].rearrange("p q t -> p (q t)"), y_codes[:, cols], y_scales[:, cols])
        nc.sync.dma_start(out_1[0].rearrange("p c r -> p (c r)").bitcast(I32), y_codes[:])
        for quad in range(4):
            queue = nc.scalar if quad % 2 == 0 else nc.sync
            queue.dma_start(
                out_2[0, 4 * quad : 4 * quad + 4, :].bitcast(I32),
                y_scales[32 * quad : 32 * quad + 4, :].bitcast(I32),
            )
